import numpy as np
import ml_dtypes


def mxq(x, axis, fmt="e4m3"):
    dtype, down = {"e4m3": (ml_dtypes.float8_e4m3fn, 7), "e5m2": (ml_dtypes.float8_e5m2, 14)}[fmt]
    v = np.moveaxis(np.asarray(x, np.float32).astype(ml_dtypes.bfloat16).astype(np.float64), axis, -1)
    blocks = v.reshape(v.shape[:-1] + (-1, 32))
    amax = np.abs(blocks).max(-1, keepdims=True)
    byte = np.maximum(np.where(amax > 0, np.frexp(amax)[1] - 1 + 127, 0) - down, 1)
    scale = np.exp2(byte - 127.0)
    codes = (blocks / scale).astype(np.float32).astype(dtype).astype(np.float64)
    return np.moveaxis((codes * scale).reshape(v.shape), -1, axis)


WIDE = False


def mx_kscale(k):
    if not WIDE:
        return np.ones(k)
    levels = np.array([10, -10, 5, -5, 0])
    if k % 512:
        return np.exp2(np.random.permutation(np.resize(levels, k // 32))).repeat(32)
    a = np.empty((k // 512, 16))
    for p in range(k // 512):
        a[p, :8] = np.random.permutation(np.resize(levels, 8))
        for g in range(8):
            far = levels[np.abs(levels - a[p, g]) >= 10]
            a[p, g + 8] = far[np.random.randint(len(far))]
    return np.exp2(a.ravel()).repeat(32)


BF16 = ml_dtypes.bfloat16


def bf(x):
    return np.asarray(x, np.float32).astype(BF16)


def f64(x):
    return np.asarray(x).astype(np.float64)


E2M1 = np.array([0.0, 0.5, 1.0, 1.5, 2.0, 3.0, 4.0, 6.0, -0.0, -0.5, -1.0, -1.5, -2.0, -3.0, -4.0, -6.0])


def pack_weight(w, fmt):
    k, n = w.shape
    w = f64(bf(w)).reshape(k // 32, 32, n)
    amax = np.abs(w).max(1)
    if fmt == "e4m3":
        byte = np.frexp(amax)[1] - 1 + 127 - 7
    else:
        mant, ex = np.frexp(amax / 6.0)
        byte = np.where(mant > 0.5, ex, ex - 1) + 127
    byte = np.clip(np.where(amax > 0, byte, 1), 1, 254)
    scaled = (w * np.exp2(127.0 - byte)[:, None, :]).reshape(k, n).astype(np.float32)
    by_word = np.ascontiguousarray(scaled.reshape(k // 512, 128, 4, n).transpose(0, 1, 3, 2))
    if fmt == "e4m3":
        words = by_word.astype(ml_dtypes.float8_e4m3fn).view(np.uint8)
    else:
        c = by_word.astype(ml_dtypes.float4_e2m1fn).view(np.uint8) & 0xF
        words = c[..., 0::2] | (c[..., 1::2] << 4)
    return np.ascontiguousarray(words), np.ascontiguousarray(byte.astype(np.uint8).reshape(k // 512, 16, n))


def unpack_weight(words, scales, fmt):
    g, p, n, _ = words.shape
    if fmt == "e4m3":
        vals = np.ascontiguousarray(words).view(ml_dtypes.float8_e4m3fn).astype(np.float64)
    else:
        nib = np.empty((g, p, n, 4), np.uint8)
        nib[..., 0::2] = words & 0xF
        nib[..., 1::2] = words >> 4
        vals = E2M1[nib]
    vals = vals * np.repeat(np.exp2(scales.astype(np.float64) - 127.0), 8, axis=1)[..., None]
    return vals.transpose(0, 1, 3, 2).reshape(g * 512, n)
def pack4(w):
    words, scales = pack_weight(w, "e2m1")
    return words.reshape(words.shape[0], 128, -1), scales


def unpack4(words, scales):
    return unpack_weight(words.reshape(words.shape[0], 128, -1, 2), scales, "e2m1")


def planes(Y):
    n, m = Y.shape
    b = f64(bf(Y)).reshape(n // 32, 32, m)
    amax = np.abs(b).max(1)
    byte = np.clip(np.where(amax > 0, np.frexp(amax)[1] - 1 + 127 - 7, 1), 1, 254)
    codes = (b * np.exp2(127.0 - byte)[:, None, :]).reshape(n, m).astype(np.float32).astype(ml_dtypes.float8_e4m3fn).view(np.uint8)
    words = codes.reshape(n // 512, 128, 4, m).transpose(0, 1, 3, 2)
    return np.ascontiguousarray(words), np.ascontiguousarray(byte.astype(np.uint8).reshape(n // 512, 16, m))


P, Q, D, S, R, F, N = 16, 8, 8, 1024, 1536, 1024, 1024


def setup_inputs():
    s = mx_kscale(R)
    t = mx_kscale(F)
    fx = np.random.uniform(-1.7, 1.7, (P, R))
    fy = np.random.uniform(-1.7, 1.7, (Q, R))
    fz = np.random.uniform(-1.7, 1.7, (D, R)) * s[None, :]
    basis = 0.35 * np.random.randn(R, F) / np.sqrt(R) / s[:, None] * t[None, :]
    x = np.random.randn(S, F) * t[None, :]
    view = 0.35 * np.random.randn(S, F) * t[None, :]
    w1_words, w1_scales = pack4(np.random.randn(F, F) / np.sqrt(F) / t[:, None])
    spread = np.exp(0.8 * np.random.randn(N))
    w2 = np.random.randn(F, N) / np.sqrt(F) * spread[None, :] / t[:, None]
    b = 0.3 * np.random.randn(N) * spread
    return {"fx": bf(fx), "fy": bf(fy), "fz": bf(fz), "basis": bf(basis), "x": bf(x), "view": bf(view),
            "w1_words": w1_words, "w1_scales": w1_scales, "w2": bf(w2), "b": bf(b)}

def reference(fx, fy, fz, basis, x, view, w1_words, w1_scales, w2, b):
    h = (f64(fx)[:, None, None, :] * f64(fy)[None, :, None, :] * f64(fz)[None, None, :, :]).reshape(S, R)
    u1 = f64(x) + (mxq(h, 1, "e4m3") @ mxq(f64(basis), 0, "e4m3"))
    u2 = u1 + f64(view) * (mxq(u1, 1, "e4m3") @ unpack4(w1_words, w1_scales))
    y = (mxq(u2, 1, "e4m3") @ mxq(f64(w2), 0, "e4m3")) + f64(b)[None, :]
    words, scales = planes(y.T)
    return y, words, scales

@@ -1,0 +1,518 @@
+from contextlib import ExitStack
+
+import concourse.mybir as mybir
+from concourse.masks import make_identity
+
+F32 = mybir.dt.float32
+BF16 = mybir.dt.bfloat16
+I32 = mybir.dt.int32
+U32 = mybir.dt.uint32
+U8 = mybir.dt.uint8
+FP8X4 = mybir.dt.float8_e4m3fn_x4
+FP4X4 = mybir.dt.float4_e2m1fn_x4
+ADD = mybir.AluOpType.add
+MULT = mybir.AluOpType.mult
+
+P = 128
+KP = 512
+S, R, F = 1024, 1536, 1024
+NI, NJ, NL = 16, 8, 8
+TILES = S // P
+RG = R // KP
+FG = F // KP
+PAIRS = TILES // 2
+FLOPS = 2 * S * F * (R + F + F)
+EARLY = 4
+ON_VECTOR = (4, 6)
+AHEAD = 5
+BEHIND = 2
+
+
+def tile_cp_radiance_shading_k1_kernel(
+    tc, fx, fy, fz, basis, x, view, w1_words, w1_scales, w2, b, out_0, out_1, out_2
+):
+    nc = tc.nc
+    with ExitStack() as ctx:
+        keep = ctx.enter_context(tc.tile_pool(name="keep", bufs=1))
+        work = ctx.enter_context(tc.tile_pool(name="work", bufs=3))
+        psum = ctx.enter_context(tc.psum_pool(name="psum", bufs=4))
+        ctx.enter_context(tc.manual_schedule())
+
+        fac = keep.tile([P, R], BF16, name="fac")
+        nc.vector.memset(fac[32:64, :].bitcast(I32), 0)
+        nc.vector.memset(fac[64:128, :].bitcast(I32), 0)
+        ident = keep.tile([P, P], F32, name="ident")
+        make_identity(nc, ident[:])
+        w1_scale = keep.tile([P, FG, F], U8, name="w1_scale", align_bytes=64)
+        nc.vector.memset(w1_scale[:].rearrange("p g n -> p (g n)").bitcast(I32), 0)
+
+        nc.sync.dma_start(out=fac[16:24, :], in_=fy)
+        nc.sync.dma_start(out=fac[24:32, :], in_=fz)
+        nc.sync.dma_start(out=fac[0:16, :], in_=fx)
+
+        def load_weight(w, g, h, name):
+            raw = work.tile([P, 4, KP], BF16, name=name, tag="raw", bufs=6)
+            nc.sync.dma_start(
+                out=raw[:], in_=w[KP * g : KP * (g + 1), KP * h : KP * (h + 1)].rearrange("(p t) n -> p t n", t=4)
+            )
+            return raw
+
+        def load_rows(a, c, name):
+            rows = keep.tile([P, 2, F], BF16, name=name)
+            nc.sync.dma_start(out=rows[:], in_=a[2 * P * c : 2 * P * (c + 1), :].rearrange("(j p) f -> p j f", p=P))
+            return rows
+
+        basis_raw = {}
+        for h in range(FG):
+            for g in range(RG):
+                basis_raw[g, h] = load_weight(basis, g, h, "basis_raw%d%d" % (g, h))
+        x_sb = {c: load_rows(x, c, "x%d" % c) for c in range(2)}
+        w1_code = keep.tile([P, FG, 2 * F], U8, name="w1_code", align_bytes=64)
+        bias = keep.tile([P, F], BF16, name="bias")
+        view_sb, w2_raw = {}, {}
+
+        def later_loads():
+            for h in range(FG):
+                for g in range(FG):
+                    w2_raw[g, h] = load_weight(w2, g, h, "w2_raw%d%d" % (g, h))
+            x_sb[2] = load_rows(x, 2, "x2")
+            for q in range(4):
+                nc.sync.dma_start(
+                    out=w1_scale[32 * q : 32 * q + 4, :, :].bitcast(I32),
+                    in_=w1_scales[:, 4 * q : 4 * q + 4, :].rearrange("g r n -> r g n").bitcast(I32),
+                )
+            nc.sync.dma_start(out=w1_code[:].bitcast(I32), in_=w1_words.rearrange("g p n -> p g n").bitcast(I32))
+            view_sb[0] = load_rows(view, 0, "view0")
+            x_sb[3] = load_rows(x, 3, "x3")
+            for c in range(1, PAIRS):
+                view_sb[c] = load_rows(view, c, "view%d" % c)
+            nc.sync.dma_start(out=bias[:], in_=b.partition_broadcast(P))
+
+        fac_words = fac[:].bitcast(F32)
+        fac_t = []
+        fyz = []
+        fac_banks = []
+        for g in range(RG):
+            fac_bank = psum.tile([P, KP], F32, name="fac_bank", tag="tr")
+            for u in range(2):
+                nc.tensor.transpose(fac_bank[:, P * u : P * (u + 1)], fac_words[:, 256 * g + u : 256 * (g + 1) : 2], ident[:])
+            fac_banks.append(fac_bank)
+
+        def axis_factors(g):
+            ft = keep.tile([P, 32, 4], BF16, name="fac_t%d" % g)
+            nc.vector.tensor_copy(
+                out=ft[:].rearrange("p r t -> p (r t)").bitcast(F32).rearrange("p (r u) -> p r u", u=2),
+                in_=fac_banks[g][:, 0 : 2 * P].rearrange("p (u r) -> p r u", u=2)[:, 0:32, :],
+            )
+            fac_t.append(ft)
+
+        def outer_yz(g):
+            yz = keep.tile([P, NJ, NL, 4], F32, name="fyz%d" % g)
+            nc.vector.tensor_tensor(
+                out=yz[:],
+                in0=fac_t[g][:, 16:24, :].unsqueeze(2).to_broadcast([P, NJ, NL, 4]),
+                in1=fac_t[g][:, 24:32, :].unsqueeze(1).to_broadcast([P, NJ, NL, 4]),
+                op=MULT,
+            )
+            fyz.append(yz)
+
+        def quantize(src, name, pool, bufs=None):
+            width = src.shape[1] // 4
+            code = pool.tile([P, width], U32, name=name + "_code", align_bytes=64, bufs=bufs)
+            scale = pool.tile([P, width], U8, name=name + "_scale", align_bytes=64, bufs=bufs)
+            nc.vector.quantize_mx(out=code[:].bitcast(FP8X4), scales=scale[:], in_=src)
+            return code, scale
+
+        def interleave(copy, raw, grouped, first, last):
+            copy(
+                out=grouped[:, 4 * first : 4 * last].rearrange("p (c i t) -> p c t i", i=4, t=4),
+                in_=raw[:, :, first:last].rearrange("p t (c i) -> p c t i", i=4),
+            )
+
+        def new_grouped():
+            return work.tile([P, KP * 4], BF16, name="grouped", align_bytes=64, bufs=4)
+
+        h_bf, h_q, basis_q, w2_q = {}, {}, {}, {}
+
+        def make_h(j, g):
+            hb = work.tile([P, 2, NJ * NL, 4], BF16, name="h_bf", align_bytes=64, bufs=4)
+            nc.vector.tensor_tensor(
+                out=hb[:],
+                in0=fyz[g][:].rearrange("p j l t -> p (j l) t").unsqueeze(1).to_broadcast([P, 2, NJ * NL, 4]),
+                in1=fac_t[g][:, 2 * j : 2 * j + 2, :].unsqueeze(2).to_broadcast([P, 2, NJ * NL, 4]),
+                op=MULT,
+            )
+            h_bf[j, g] = hb
+
+        def quantize_h(j, g):
+            h_q[j, g] = quantize(h_bf[j, g][:].rearrange("p i m t -> p (i m t)"), "h%d%d" % (j, g), keep)
+
+        def mx_passes(acts, weights):
+            bank = psum.tile([P, KP], F32, name="mx_bank", tag="mx")
+            for n in range(len(acts)):
+                nc.tensor.matmul_mx(
+                    out=bank[:],
+                    lhsT=acts[n][0].bitcast(FP8X4),
+                    lhsT_scale=acts[n][1],
+                    rhs=weights[n][0],
+                    rhs_scale=weights[n][1],
+                    start=(n == 0),
+                    stop=(n == len(acts) - 1),
+                )
+            return bank
+
+        def act_passes(q):
+            return [(q[0][:, P * g : P * (g + 1)], q[1][:, P * g : P * (g + 1)]) for g in range(FG)]
+
+        def sorted_view(ap):
+            return ap.rearrange("p (t c i) -> p c t i", t=4, i=4)
+
+        def plain_view(ap):
+            return ap.rearrange("p (c i t) -> p c t i", t=4, i=4)
+
+        bank1, bank2, bank3, tr1, tr2, tr3 = {}, {}, {}, {}, {}, {}
+        u1, mod, y, u1_bf, u2_bf, y_bf, yt_bf, u1_q, u2_q = {}, {}, {}, {}, {}, {}, {}, {}, {}
+        u1_w, u2_w = {}, {}
+        y_code = {}
+        y_scale = keep.tile([P, FG, S], U8, name="y_scale", align_bytes=64)
+
+        def live(j):
+            return 0 <= j < TILES
+
+        def stage1(j, h):
+            bank1[j, h] = mx_passes(
+                [(h_q[j, g][0][:], h_q[j, g][1][:]) for g in range(RG)],
+                [(basis_q[g, h][0][:].bitcast(FP8X4), basis_q[g, h][1][:]) for g in range(RG)],
+            )
+
+        def add_x(j, h):
+            if h == 0:
+                u1[j] = work.tile([P, F], F32, name="u1", bufs=TILES)
+            cols = slice(KP * h, KP * (h + 1))
+            nc.vector.tensor_tensor(
+                out=sorted_view(u1[j][:, cols]),
+                in0=plain_view(bank1[j, h][:]),
+                in1=plain_view(x_sb[j // 2][:, j % 2, cols]),
+                op=ADD,
+            )
+
+        def add_u2(j, g):
+            if g == 0:
+                u2_w[j] = work.tile([P, F], BF16, name="u2_w", bufs=2)
+            cols = slice(KP * g, KP * (g + 1))
+            nc.vector.tensor_tensor(
+                out=u2_w[j][:, cols].rearrange("p (u q e) -> p u q e", u=2, e=2),
+                in0=u1[j][:, cols].rearrange("p (u e q) -> p u q e", u=2, e=2),
+                in1=mod[j][:, cols].rearrange("p (u e q) -> p u q e", u=2, e=2),
+                op=ADD,
+            )
+
+        def turn_u1(j, g):
+            bank = psum.tile([P, KP], F32, name="tr_bank", tag="tr")
+            for t in range(4):
+                cols = slice(KP * g + P * t, KP * g + P * (t + 1))
+                nc.tensor.transpose(bank[:, P * t : P * (t + 1)], u1[j][:, cols], ident[:])
+            tr1[j, g] = bank
+            round_turned(u1_bf, tr1, j, g, "u1_bf", 5)
+
+        def turn_words(src, groups=range(FG)):
+            bank = psum.tile([P, KP], F32, name="tr_bank", tag="tr")
+            words = src[:].bitcast(F32)
+            for g in groups:
+                for n in (2 * g, 2 * g + 1):
+                    nc.tensor.transpose(bank[:, P * n : P * (n + 1)], words[:, P * n : P * (n + 1)], ident[:])
+            return bank
+
+        def gather_words(bank, name):
+            dst = work.tile([P, F], BF16, name=name, align_bytes=64, bufs=2)
+            nc.scalar.copy(
+                out=dst[:].bitcast(F32).rearrange("p (g s u) -> p g s u", g=FG, u=2),
+                in_=bank[:].rearrange("p (g u s) -> p g s u", g=FG, u=2),
+            )
+            return dst
+
+        def gather_group(bank, dst, g):
+            nc.scalar.copy(
+                out=dst[:, KP * g : KP * (g + 1)].bitcast(F32).rearrange("p (s u) -> p s u", u=2),
+                in_=bank[:, 2 * P * g : 2 * P * (g + 1)].rearrange("p (u s) -> p s u", u=2),
+            )
+
+        def round_turned(dst, banks, j, g, name, bufs):
+            if g == 0:
+                dst[j] = work.tile([P, F], BF16, name=name, align_bytes=64, bufs=bufs)
+            nc.scalar.copy(
+                out=dst[j][:, KP * g : KP * (g + 1)].rearrange("p (s t) -> p s t", t=4),
+                in_=banks[j, g][:].rearrange("p (t s) -> p s t", t=4),
+            )
+
+        def stage2(j, h):
+            bank2[j, h] = mx_passes(
+                act_passes(u1_q[j]),
+                [
+                    (w1_code[:, g, 2 * KP * h : 2 * KP * (h + 1)].bitcast(FP4X4), w1_scale[:, g, KP * h : KP * (h + 1)])
+                    for g in range(FG)
+                ],
+            )
+
+        def mul_view(j, h):
+            if h == 0:
+                mod[j] = work.tile([P, F], F32, name="mod", bufs=2)
+            cols = slice(KP * h, KP * (h + 1))
+            nc.vector.tensor_tensor(
+                out=sorted_view(mod[j][:, cols]),
+                in0=plain_view(bank2[j, h][:]),
+                in1=plain_view(view_sb[j // 2][:, j % 2, cols]),
+                op=MULT,
+            )
+
+        def turn_u2(j, g):
+            bank = psum.tile([P, KP], F32, name="tr_bank", tag="tr")
+            for t in range(4):
+                cols = slice(KP * g + P * t, KP * g + P * (t + 1))
+                out = bank[:, P * t : P * (t + 1)]
+                nc.tensor.matmul(out, lhsT=u1[j][:, cols], rhs=ident[:], is_transpose=True, start=True, stop=False)
+                nc.tensor.matmul(out, lhsT=mod[j][:, cols], rhs=ident[:], is_transpose=True, start=False, stop=True)
+            tr2[j, g] = bank
+
+        def stage3(j, h):
+            bank3[j, h] = mx_passes(
+                act_passes(u2_q[j]),
+                [(w2_q[g, h][0][:].bitcast(FP8X4), w2_q[g, h][1][:]) for g in range(FG)],
+            )
+
+        def add_bias(j, h):
+            if h == 0:
+                y[j] = work.tile([P, F], F32, name="y")
+            cols = slice(KP * h, KP * (h + 1))
+            nc.vector.tensor_tensor(out=y[j][:, cols], in0=bank3[j, h][:], in1=bias[:, cols], op=ADD)
+            if h == FG - 1:
+                nc.sync.dma_start(out=out_0[P * j : P * (j + 1), :], in_=y[j][:])
+
+        def round_y(j, g, copy):
+            if g == 0:
+                y_bf[j] = work.tile([P, F], BF16, name="y_bf", bufs=3)
+            cols = slice(KP * g, KP * (g + 1))
+            copy(
+                out=y_bf[j][:, cols].rearrange("p (u q e) -> p u q e", u=2, e=2),
+                in_=y[j][:, cols].rearrange("p (q u e) -> p u q e", u=2, e=2),
+            )
+
+        def quantize_y(j, groups=range(FG)):
+            first, count = (j - j % 2, 2) if j < TILES - 2 else (j, 1)
+            if first not in y_code:
+                y_code[first] = work.tile([P, FG, count * P], U32, name="y_code", align_bytes=64)
+            for g in groups:
+                nc.vector.quantize_mx(
+                    out=y_code[first][:, g, P * (j - first) : P * (j - first + 1)].bitcast(FP8X4),
+                    scales=y_scale[:, g, P * j : P * (j + 1)],
+                    in_=yt_bf[j][:, KP * g : KP * (g + 1)],
+                )
+            if j == first + count - 1 and FG - 1 in groups:
+                nc.sync.dma_start(
+                    out=out_1.rearrange("g p m t -> p g (m t)").bitcast(I32)[:, :, P * first : P * (j + 1)],
+                    in_=y_code[first][:].bitcast(I32),
+                )
+
+        h_todo = [(j, g) for j in range(TILES) for g in range(RG)]
+        w2_todo = [(g, h, part) for h in range(FG) for g in range(FG) for part in range(2)]
+        h_made, w2_made, w2_grouped, basis_grouped = [], [], {}, {}
+
+        def next_h():
+            if h_todo:
+                piece = h_todo.pop(0)
+                make_h(*piece)
+                h_made.append(piece)
+
+        def finish_h():
+            while h_made:
+                quantize_h(*h_made.pop(0))
+
+        def quantize_basis(g, h):
+            basis_q[g, h] = quantize(basis_grouped[g, h][:], "basis%d%d" % (g, h), keep)
+
+        def group_basis(g, h):
+            basis_grouped[g, h] = new_grouped()
+            interleave(nc.scalar.copy, basis_raw[g, h], basis_grouped[g, h], 0, KP)
+
+        def next_w2():
+            if w2_todo:
+                g, h, part = w2_todo.pop(0)
+                if part == 0:
+                    w2_grouped[g, h] = new_grouped()
+                interleave(nc.scalar.copy, w2_raw[g, h], w2_grouped[g, h], part * KP // 2, (part + 1) * KP // 2)
+                if part == 1:
+                    w2_made.append((g, h))
+
+        def finish_w2():
+            while w2_made:
+                piece = w2_made.pop(0)
+                w2_q[piece] = quantize(w2_grouped[piece][:], "w2_%d%d" % piece, keep)
+
+        def quantize_u1(j):
+            u1_q[j] = quantize(u1_bf[j][:], "u1", work, bufs=TILES)
+
+        def quantize_u2(j):
+            u2_q[j] = quantize(u2_bf[j][:], "u2", work, bufs=4)
+
+        def h_run(n):
+            for k in range(n):
+                next_h()
+            finish_h()
+
+        for g in range(RG):
+            group_basis(g, 0)
+        group_basis(0, 1)
+        axis_factors(0)
+        axis_factors(1)
+        outer_yz(0)
+        axis_factors(2)
+        outer_yz(1)
+        next_h()
+        outer_yz(2)
+        h_run(2)
+        quantize_basis(0, 0)
+        group_basis(1, 1)
+        next_h()
+        quantize_basis(1, 0)
+        group_basis(2, 1)
+        later_loads()
+        h_run(2)
+        next_h()
+        quantize_basis(2, 0)
+        stage1(0, 0)
+        stage1(1, 0)
+        h_run(2)
+        stage1(2, 0)
+        quantize_basis(0, 1)
+        add_x(0, 0)
+        add_x(1, 0)
+        h_run(2)
+        quantize_basis(1, 1)
+        h_run(1)
+        stage1(3, 0)
+        add_x(2, 0)
+        next_w2()
+        turn_u1(0, 0)
+        turn_u1(1, 0)
+        quantize_basis(2, 1)
+        next_h()
+        add_x(3, 0)
+        for j in range(EARLY):
+            stage1(j, 1)
+        next_w2()
+        next_h()
+        add_x(0, 1)
+        h_run(1)
+        add_x(1, 1)
+        next_w2()
+        turn_u1(0, 1)
+        turn_u1(2, 0)
+        turn_u1(1, 1)
+        turn_u1(3, 0)
+        add_x(2, 1)
+        add_x(3, 1)
+        next_w2()
+        stage1(4, 0)
+        stage1(4, 1)
+        next_h()
+        quantize_u1(0)
+        next_h()
+        quantize_u1(1)
+        add_x(4, 0)
+        h_run(1)
+        add_x(4, 1)
+        turn_u1(2, 1)
+        turn_u1(3, 1)
+        next_w2()
+
+        def finish_y(j):
+            yt_bf[j] = gather_words(turn_words(y_bf[j]), "yt_bf")
+
+        for a in range(TILES):
+            j, c = a + AHEAD, a - BEHIND
+            d, e = c - 1, c - 2
+            stage2(a, 0)
+            stage2(a, 1)
+            if live(j):
+                stage1(j, 0)
+                stage1(j, 1)
+            if a == 0:
+                quantize_u1(j - 3)
+            if live(j - 2):
+                quantize_u1(j - 2)
+            next_h()
+            finish_w2()
+            if live(e):
+                quantize_y(e)
+            if a - 2 in ON_VECTOR:
+                quantize_u2(a - 2)
+            if live(d):
+                round_y(d, 0, nc.scalar.copy)
+                round_y(d, 1, nc.scalar.copy)
+            next_w2()
+            mul_view(a, 0)
+            mul_view(a, 1)
+            if live(c):
+                stage3(c, 0)
+                stage3(c, 1)
+            if live(a - 1) and a - 1 not in ON_VECTOR:
+                quantize_u2(a - 1)
+            if live(j):
+                add_x(j, 0)
+            next_h()
+            if live(j):
+                add_x(j, 1)
+            if live(c):
+                add_bias(c, 0)
+                add_bias(c, 1)
+            if a in ON_VECTOR:
+                add_u2(a, 0)
+                add_u2(a, 1)
+            h_run(1)
+            if a - 1 in ON_VECTOR:
+                u2_bf[a - 1] = gather_words(turn_words(u2_w[a - 1]), "u2_bf")
+            if live(j - 1):
+                turn_u1(j - 1, 0)
+                turn_u1(j - 1, 1)
+            if live(d):
+                finish_y(d)
+            if a not in ON_VECTOR:
+                for g in range(FG):
+                    turn_u2(a, g)
+                    round_turned(u2_bf, tr2, a, g, "u2_bf", 2)
+            next_w2()
+
+        last = TILES - 1
+        if last - 1 not in u2_q:
+            quantize_u2(last - 1)
+        stage3(last - 1, 0)
+        stage3(last - 1, 1)
+        quantize_y(last - 3)
+        add_bias(last - 1, 0)
+        quantize_u2(last)
+        stage3(last, 0)
+        stage3(last, 1)
+        add_bias(last - 1, 1)
+        round_y(last - 2, 0, nc.scalar.copy)
+        round_y(last - 2, 1, nc.scalar.copy)
+        round_y(last - 1, 0, nc.scalar.copy)
+        add_bias(last, 0)
+        round_y(last - 1, 1, nc.vector.tensor_copy)
+        add_bias(last, 1)
+        finish_y(last - 2)
+        round_y(last, 0, nc.vector.tensor_copy)
+        round_y(last, 1, nc.vector.tensor_copy)
+        finish_y(last - 1)
+        quantize_y(last - 2)
+        yt_bf[last] = work.tile([P, F], BF16, name="yt_bf", align_bytes=64, bufs=2)
+        for g in range(FG):
+            gather_group(turn_words(y_bf[last], [g]), yt_bf[last], g)
+        quantize_y(last - 1)
+        for g in range(FG):
+            quantize_y(last, [g])
+
+        for q in range(4):
+            nc.sync.dma_start(
+                out=out_2[:, 4 * q : 4 * q + 4, :].rearrange("g r m -> r g m").bitcast(I32),
+                in_=y_scale[32 * q : 32 * q + 4, :, :].bitcast(I32),
+            )

@@ -24,8 +24,9 @@ PAIRS = TILES // 2
 FLOPS = 2 * S * F * (R + F + F)
 EARLY = 4
 ON_VECTOR = (4, 6)
-AHEAD = 5
-BEHIND = 2
+ROUNDED_FIRST = (4, 5, 6, 7)
+STAGE1_AT = {0: 5, 2: 6, 4: 7}
+STAGE3_AT = {4: (0,), 5: (1, 2), 6: (3,), 7: (4, 5)}
 
 
 def tile_cp_radiance_shading_k1_kernel(
@@ -130,22 +131,25 @@ def tile_cp_radiance_shading_k1_kernel(
             )
 
         def new_grouped():
-            return work.tile([P, KP * 4], BF16, name="grouped", align_bytes=64, bufs=4)
+            return work.tile([P, KP * 4], BF16, name="grouped", align_bytes=64, bufs=3)
 
         h_bf, h_q, basis_q, w2_q = {}, {}, {}, {}
 
-        def make_h(j, g):
-            hb = work.tile([P, 2, NJ * NL, 4], BF16, name="h_bf", align_bytes=64, bufs=4)
+        def make_h(first, count, g):
+            hb = work.tile([P, 2 * count, NJ * NL, 4], BF16, name="h_bf", align_bytes=64, bufs=3)
+            shape = [P, 2 * count, NJ * NL, 4]
             nc.vector.tensor_tensor(
                 out=hb[:],
-                in0=fyz[g][:].rearrange("p j l t -> p (j l) t").unsqueeze(1).to_broadcast([P, 2, NJ * NL, 4]),
-                in1=fac_t[g][:, 2 * j : 2 * j + 2, :].unsqueeze(2).to_broadcast([P, 2, NJ * NL, 4]),
+                in0=fyz[g][:].rearrange("p j l t -> p (j l) t").unsqueeze(1).to_broadcast(shape),
+                in1=fac_t[g][:, 2 * first : 2 * (first + count), :].unsqueeze(2).to_broadcast(shape),
                 op=MULT,
             )
-            h_bf[j, g] = hb
+            h_bf[first, g] = hb
 
-        def quantize_h(j, g):
-            h_q[j, g] = quantize(h_bf[j, g][:].rearrange("p i m t -> p (i m t)"), "h%d%d" % (j, g), keep)
+        def quantize_h(first, count, g):
+            code, scale = quantize(h_bf[first, g][:].rearrange("p i m t -> p (i m t)"), "h", work, bufs=2 * RG + 1)
+            for k in range(count):
+                h_q[first + k, g] = (code[:, P * k : P * (k + 1)], scale[:, P * k : P * (k + 1)])
 
         def mx_passes(acts, weights):
             bank = psum.tile([P, KP], F32, name="mx_bank", tag="mx")
@@ -164,10 +168,14 @@ def tile_cp_radiance_shading_k1_kernel(
         def act_passes(q):
             return [(q[0][:, P * g : P * (g + 1)], q[1][:, P * g : P * (g + 1)]) for g in range(FG)]
 
-        def sorted_view(ap):
+        def sorted_view(ap, j):
+            if j in ON_VECTOR:
+                return ap.rearrange("p (u q e) -> p u q e", u=2, e=2)
             return ap.rearrange("p (t c i) -> p c t i", t=4, i=4)
 
-        def plain_view(ap):
+        def plain_view(ap, j):
+            if j in ON_VECTOR:
+                return ap.rearrange("p (q u e) -> p u q e", u=2, e=2)
             return ap.rearrange("p (c i t) -> p c t i", t=4, i=4)
 
         bank1, bank2, bank3, tr1, tr2, tr3 = {}, {}, {}, {}, {}, {}
@@ -181,18 +189,18 @@ def tile_cp_radiance_shading_k1_kernel(
 
         def stage1(j, h):
             bank1[j, h] = mx_passes(
-                [(h_q[j, g][0][:], h_q[j, g][1][:]) for g in range(RG)],
+                [h_q[j, g] for g in range(RG)],
                 [(basis_q[g, h][0][:].bitcast(FP8X4), basis_q[g, h][1][:]) for g in range(RG)],
             )
 
         def add_x(j, h):
             if h == 0:
-                u1[j] = work.tile([P, F], F32, name="u1", bufs=TILES)
+                u1[j] = work.tile([P, F], F32, name="u1", bufs=6)
             cols = slice(KP * h, KP * (h + 1))
             nc.vector.tensor_tensor(
-                out=sorted_view(u1[j][:, cols]),
-                in0=plain_view(bank1[j, h][:]),
-                in1=plain_view(x_sb[j // 2][:, j % 2, cols]),
+                out=sorted_view(u1[j][:, cols], j),
+                in0=plain_view(bank1[j, h][:], j),
+                in1=plain_view(x_sb[j // 2][:, j % 2, cols], j),
                 op=ADD,
             )
 
@@ -200,14 +208,21 @@ def tile_cp_radiance_shading_k1_kernel(
             if g == 0:
                 u2_w[j] = work.tile([P, F], BF16, name="u2_w", bufs=2)
             cols = slice(KP * g, KP * (g + 1))
-            nc.vector.tensor_tensor(
-                out=u2_w[j][:, cols].rearrange("p (u q e) -> p u q e", u=2, e=2),
-                in0=u1[j][:, cols].rearrange("p (u e q) -> p u q e", u=2, e=2),
-                in1=mod[j][:, cols].rearrange("p (u e q) -> p u q e", u=2, e=2),
-                op=ADD,
-            )
+            nc.vector.tensor_tensor(out=u2_w[j][:, cols], in0=u1[j][:, cols], in1=mod[j][:, cols], op=ADD)
 
-        def turn_u1(j, g):
+        def round_u1(j, g):
+            if g == 0:
+                u1_w[j] = work.tile([P, F], BF16, name="u1_w", bufs=2)
+            cols = slice(KP * g, KP * (g + 1))
+            if j in ON_VECTOR:
+                nc.scalar.copy(out=u1_w[j][:, cols], in_=u1[j][:, cols])
+            else:
+                nc.scalar.copy(
+                    out=u1_w[j][:, cols].rearrange("p (u q e) -> p u q e", u=2, e=2),
+                    in_=u1[j][:, cols].rearrange("p (u e q) -> p u q e", u=2, e=2),
+                )
+
+        def turn_u1_half(j, g):
             bank = psum.tile([P, KP], F32, name="tr_bank", tag="tr")
             for t in range(4):
                 cols = slice(KP * g + P * t, KP * g + P * (t + 1))
@@ -223,18 +238,27 @@ def tile_cp_radiance_shading_k1_kernel(
                     nc.tensor.transpose(bank[:, P * n : P * (n + 1)], words[:, P * n : P * (n + 1)], ident[:])
             return bank
 
-        def gather_words(bank, name):
-            dst = work.tile([P, F], BF16, name=name, align_bytes=64, bufs=2)
+        def gather_words(bank, name, bufs=2):
+            dst = work.tile([P, F], BF16, name=name, align_bytes=64, bufs=bufs)
             nc.scalar.copy(
                 out=dst[:].bitcast(F32).rearrange("p (g s u) -> p g s u", g=FG, u=2),
                 in_=bank[:].rearrange("p (g u s) -> p g s u", g=FG, u=2),
             )
             return dst
 
-        def gather_group(bank, dst, g):
+        def plane_batch(j):
+            return (j - j % 2, 2) if j < TILES - 2 else (j, 1)
+
+        def gather_y(bank, j, groups):
+            first, count = plane_batch(j)
+            if first not in yt_bf:
+                yt_bf[first] = work.tile([P, FG, count * KP], BF16, name="yt_bf", align_bytes=64, bufs=3)
+            gs = slice(groups[0], groups[-1] + 1)
             nc.scalar.copy(
-                out=dst[:, KP * g : KP * (g + 1)].bitcast(F32).rearrange("p (s u) -> p s u", u=2),
-                in_=bank[:, 2 * P * g : 2 * P * (g + 1)].rearrange("p (u s) -> p s u", u=2),
+                out=yt_bf[first][:, gs, KP * (j - first) : KP * (j - first + 1)]
+                .bitcast(F32)
+                .rearrange("p g (s u) -> p g s u", u=2),
+                in_=bank[:].rearrange("p (g u s) -> p g s u", g=FG, u=2)[:, gs, :, :],
             )
 
         def round_turned(dst, banks, j, g, name, bufs):
@@ -256,12 +280,12 @@ def tile_cp_radiance_shading_k1_kernel(
 
         def mul_view(j, h):
             if h == 0:
-                mod[j] = work.tile([P, F], F32, name="mod", bufs=2)
+                mod[j] = work.tile([P, F], F32, name="mod", bufs=3)
             cols = slice(KP * h, KP * (h + 1))
             nc.vector.tensor_tensor(
-                out=sorted_view(mod[j][:, cols]),
-                in0=plain_view(bank2[j, h][:]),
-                in1=plain_view(view_sb[j // 2][:, j % 2, cols]),
+                out=sorted_view(mod[j][:, cols], j),
+                in0=plain_view(bank2[j, h][:], j),
+                in1=plain_view(view_sb[j // 2][:, j % 2, cols], j),
                 op=MULT,
             )
 
@@ -282,7 +306,7 @@ def tile_cp_radiance_shading_k1_kernel(
 
         def add_bias(j, h):
             if h == 0:
-                y[j] = work.tile([P, F], F32, name="y")
+                y[j] = work.tile([P, F], F32, name="y", bufs=3)
             cols = slice(KP * h, KP * (h + 1))
             nc.vector.tensor_tensor(out=y[j][:, cols], in0=bank3[j, h][:], in1=bias[:, cols], op=ADD)
             if h == FG - 1:
@@ -290,7 +314,7 @@ def tile_cp_radiance_shading_k1_kernel(
 
         def round_y(j, g, copy):
             if g == 0:
-                y_bf[j] = work.tile([P, F], BF16, name="y_bf", bufs=3)
+                y_bf[j] = work.tile([P, F], BF16, name="y_bf", bufs=4)
             cols = slice(KP * g, KP * (g + 1))
             copy(
                 out=y_bf[j][:, cols].rearrange("p (u q e) -> p u q e", u=2, e=2),
@@ -298,22 +322,24 @@ def tile_cp_radiance_shading_k1_kernel(
             )
 
         def quantize_y(j, groups=range(FG)):
-            first, count = (j - j % 2, 2) if j < TILES - 2 else (j, 1)
+            first, count = plane_batch(j)
+            if j != first + count - 1:
+                return
             if first not in y_code:
                 y_code[first] = work.tile([P, FG, count * P], U32, name="y_code", align_bytes=64)
             for g in groups:
                 nc.vector.quantize_mx(
-                    out=y_code[first][:, g, P * (j - first) : P * (j - first + 1)].bitcast(FP8X4),
-                    scales=y_scale[:, g, P * j : P * (j + 1)],
-                    in_=yt_bf[j][:, KP * g : KP * (g + 1)],
+                    out=y_code[first][:, g, :].bitcast(FP8X4),
+                    scales=y_scale[:, g, P * first : P * (j + 1)],
+                    in_=yt_bf[first][:, g, :],
                 )
-            if j == first + count - 1 and FG - 1 in groups:
+            if FG - 1 in groups:
                 nc.sync.dma_start(
                     out=out_1.rearrange("g p m t -> p g (m t)").bitcast(I32)[:, :, P * first : P * (j + 1)],
                     in_=y_code[first][:].bitcast(I32),
                 )
 
-        h_todo = [(j, g) for j in range(TILES) for g in range(RG)]
+        h_todo = [(j, n, g) for j, n in ((0, 2), (2, 2), (4, 2), (6, 1), (7, 1)) for g in range(RG)]
         w2_todo = [(g, h, part) for h in range(FG) for g in range(FG) for part in range(2)]
         h_made, w2_made, w2_grouped, basis_grouped = [], [], {}, {}
 
@@ -348,11 +374,14 @@ def tile_cp_radiance_shading_k1_kernel(
                 piece = w2_made.pop(0)
                 w2_q[piece] = quantize(w2_grouped[piece][:], "w2_%d%d" % piece, keep)
 
+        def turn_u1(j):
+            u1_bf[j] = gather_words(turn_words(u1_w[j]), "u1_bf", 5)
+
         def quantize_u1(j):
-            u1_q[j] = quantize(u1_bf[j][:], "u1", work, bufs=TILES)
+            u1_q[j] = quantize(u1_bf[j][:], "u1", work, bufs=6)
 
         def quantize_u2(j):
-            u2_q[j] = quantize(u2_bf[j][:], "u2", work, bufs=4)
+            u2_q[j] = quantize(u2_bf[j][:], "u2", work, bufs=5)
 
         def h_run(n):
             for k in range(n):
@@ -361,158 +390,173 @@ def tile_cp_radiance_shading_k1_kernel(
 
         for g in range(RG):
             group_basis(g, 0)
-        group_basis(0, 1)
         axis_factors(0)
-        axis_factors(1)
         outer_yz(0)
+        axis_factors(1)
+        next_h()
         axis_factors(2)
         outer_yz(1)
-        next_h()
         outer_yz(2)
-        h_run(2)
+        next_h()
         quantize_basis(0, 0)
-        group_basis(1, 1)
+        group_basis(0, 1)
+        finish_h()
         next_h()
         quantize_basis(1, 0)
-        group_basis(2, 1)
-        later_loads()
-        h_run(2)
+        group_basis(1, 1)
+        finish_h()
         next_h()
         quantize_basis(2, 0)
+        group_basis(2, 1)
+        later_loads()
         stage1(0, 0)
         stage1(1, 0)
-        h_run(2)
-        stage1(2, 0)
+        finish_h()
+        next_h()
         quantize_basis(0, 1)
+        finish_h()
+        next_h()
         add_x(0, 0)
-        add_x(1, 0)
-        h_run(2)
-        quantize_basis(1, 1)
-        h_run(1)
+        finish_h()
+        stage1(2, 0)
         stage1(3, 0)
-        add_x(2, 0)
-        next_w2()
-        turn_u1(0, 0)
-        turn_u1(1, 0)
+        quantize_basis(1, 1)
+        add_x(1, 0)
+        next_h()
+        turn_u1_half(0, 0)
+        turn_u1_half(1, 0)
         quantize_basis(2, 1)
-        next_h()
+        finish_h()
+        next_w2()
+        stage1(0, 1)
+        stage1(1, 1)
+        add_x(2, 0)
         add_x(3, 0)
-        for j in range(EARLY):
-            stage1(j, 1)
+        stage1(2, 1)
+        stage1(3, 1)
         next_w2()
-        next_h()
         add_x(0, 1)
-        h_run(1)
+        next_h()
         add_x(1, 1)
-        next_w2()
-        turn_u1(0, 1)
-        turn_u1(2, 0)
-        turn_u1(1, 1)
-        turn_u1(3, 0)
+        next_h()
+        finish_h()
         add_x(2, 1)
         add_x(3, 1)
+        turn_u1_half(0, 1)
+        turn_u1_half(2, 0)
+        turn_u1_half(1, 1)
+        turn_u1_half(3, 0)
         next_w2()
         stage1(4, 0)
         stage1(4, 1)
-        next_h()
         quantize_u1(0)
-        next_h()
-        quantize_u1(1)
         add_x(4, 0)
-        h_run(1)
+        finish_w2()
+        quantize_u1(1)
         add_x(4, 1)
-        turn_u1(2, 1)
-        turn_u1(3, 1)
+        turn_u1_half(2, 1)
+        turn_u1_half(3, 1)
         next_w2()
 
         def finish_y(j):
-            yt_bf[j] = gather_words(turn_words(y_bf[j]), "yt_bf")
+            gather_y(turn_words(y_bf[j]), j, range(FG))
 
+        def turn_sum(k):
+            if k in ON_VECTOR:
+                u2_bf[k] = gather_words(turn_words(u2_w[k]), "u2_bf")
+            else:
+                for g in range(FG):
+                    turn_u2(k, g)
+                    round_turned(u2_bf, tr2, k, g, "u2_bf", 2)
+
+        biased, gathered, added, waiting = [], [], [4], [2, 3]
         for a in range(TILES):
-            j, c = a + AHEAD, a - BEHIND
-            d, e = c - 1, c - 2
+            j = STAGE1_AT.get(a)
             stage2(a, 0)
             stage2(a, 1)
-            if live(j):
-                stage1(j, 0)
-                stage1(j, 1)
-            if a == 0:
-                quantize_u1(j - 3)
-            if live(j - 2):
-                quantize_u1(j - 2)
-            next_h()
-            finish_w2()
-            if live(e):
-                quantize_y(e)
-            if a - 2 in ON_VECTOR:
-                quantize_u2(a - 2)
-            if live(d):
-                round_y(d, 0, nc.scalar.copy)
-                round_y(d, 1, nc.scalar.copy)
+            for k in added:
+                round_u1(k, 0)
+                round_u1(k, 1)
+            for k in biased:
+                round_y(k, 0, nc.scalar.copy)
+                round_y(k, 1, nc.scalar.copy)
             next_w2()
+            rounded, added = added, []
+            turned, biased = biased, []
             mul_view(a, 0)
             mul_view(a, 1)
-            if live(c):
+            if j:
+                stage1(j, 0)
+                stage1(j, 1)
+            if waiting:
+                quantize_u1(waiting.pop(0))
+            if j:
+                add_x(j, 0)
+            if live(a - 2):
+                quantize_u2(a - 2)
+            next_h()
+            if j:
+                add_x(j, 1)
+                added.append(j)
+            finish_w2()
+            for c in STAGE3_AT.get(a, ()):
                 stage3(c, 0)
                 stage3(c, 1)
-            if live(a - 1) and a - 1 not in ON_VECTOR:
-                quantize_u2(a - 1)
-            if live(j):
-                add_x(j, 0)
-            next_h()
-            if live(j):
-                add_x(j, 1)
-            if live(c):
                 add_bias(c, 0)
                 add_bias(c, 1)
+                biased.append(c)
+            if j:
+                next_h()
+            for k in gathered:
+                quantize_y(k)
             if a in ON_VECTOR:
                 add_u2(a, 0)
                 add_u2(a, 1)
-            h_run(1)
-            if a - 1 in ON_VECTOR:
-                u2_bf[a - 1] = gather_words(turn_words(u2_w[a - 1]), "u2_bf")
-            if live(j - 1):
-                turn_u1(j - 1, 0)
-                turn_u1(j - 1, 1)
-            if live(d):
-                finish_y(d)
-            if a not in ON_VECTOR:
-                for g in range(FG):
-                    turn_u2(a, g)
-                    round_turned(u2_bf, tr2, a, g, "u2_bf", 2)
-            next_w2()
+            finish_h()
+            if live(a - 1):
+                turn_sum(a - 1)
+            for k in rounded:
+                turn_u1(k)
+                waiting.append(k)
+            for k in turned:
+                finish_y(k)
+            gathered = turned
 
         last = TILES - 1
-        if last - 1 not in u2_q:
-            quantize_u2(last - 1)
+        turn_sum(last)
+        quantize_u2(last - 1)
+        round_y(last - 3, 0, nc.scalar.copy)
+        round_y(last - 3, 1, nc.scalar.copy)
+        round_y(last - 2, 0, nc.vector.tensor_copy)
+        round_y(last - 2, 1, nc.vector.tensor_copy)
         stage3(last - 1, 0)
         stage3(last - 1, 1)
-        quantize_y(last - 3)
-        add_bias(last - 1, 0)
+        for k in gathered:
+            quantize_y(k)
         quantize_u2(last)
+        add_bias(last - 1, 0)
+        add_bias(last - 1, 1)
         stage3(last, 0)
         stage3(last, 1)
-        add_bias(last - 1, 1)
-        round_y(last - 2, 0, nc.scalar.copy)
-        round_y(last - 2, 1, nc.scalar.copy)
         round_y(last - 1, 0, nc.scalar.copy)
         add_bias(last, 0)
         round_y(last - 1, 1, nc.vector.tensor_copy)
         add_bias(last, 1)
-        finish_y(last - 2)
+        for k in biased:
+            finish_y(k)
         round_y(last, 0, nc.vector.tensor_copy)
         round_y(last, 1, nc.vector.tensor_copy)
         finish_y(last - 1)
-        quantize_y(last - 2)
-        yt_bf[last] = work.tile([P, F], BF16, name="yt_bf", align_bytes=64, bufs=2)
         for g in range(FG):
-            gather_group(turn_words(y_bf[last], [g]), yt_bf[last], g)
-        quantize_y(last - 1)
+            gather_y(turn_words(y_bf[last], [g]), last, [g])
+        for k in biased + [last - 1]:
+            quantize_y(k)
         for g in range(FG):
             quantize_y(last, [g])
 
         for q in range(4):
-            nc.sync.dma_start(
+            queue = nc.sync if q < 2 else nc.scalar
+            queue.dma_start(
                 out=out_2[:, 4 * q : 4 * q + 4, :].rearrange("g r m -> r g m").bitcast(I32),
                 in_=y_scale[32 * q : 32 * q + 4, :, :].bitcast(I32),
             )

@@ -23,7 +23,7 @@ FG = F // KP
 PAIRS = TILES // 2
 FLOPS = 2 * S * F * (R + F + F)
 EARLY = 4
-ON_VECTOR = (4, 6)
+ON_VECTOR = (4, 5, 6)
 ROUNDED_FIRST = (4, 5, 6, 7)
 STAGE1_AT = {0: 5, 2: 6, 4: 7}
 STAGE3_AT = {4: (0,), 5: (1, 2), 6: (3,), 7: (4, 5)}
@@ -513,6 +513,9 @@ def tile_cp_radiance_shading_k1_kernel(
                 add_u2(a, 0)
                 add_u2(a, 1)
             finish_h()
+            if a == TILES - 1:
+                round_y(biased[0], 0, nc.scalar.copy)
+                round_y(biased[0], 1, nc.scalar.copy)
             if live(a - 1):
                 turn_sum(a - 1)
             for k in rounded:
@@ -525,10 +528,9 @@ def tile_cp_radiance_shading_k1_kernel(
         last = TILES - 1
         turn_sum(last)
         quantize_u2(last - 1)
-        round_y(last - 3, 0, nc.scalar.copy)
-        round_y(last - 3, 1, nc.scalar.copy)
         round_y(last - 2, 0, nc.vector.tensor_copy)
         round_y(last - 2, 1, nc.vector.tensor_copy)
+        finish_y(last - 3)
         stage3(last - 1, 0)
         stage3(last - 1, 1)
         for k in gathered:
@@ -539,18 +541,17 @@ def tile_cp_radiance_shading_k1_kernel(
         stage3(last, 0)
         stage3(last, 1)
         round_y(last - 1, 0, nc.scalar.copy)
+        round_y(last - 1, 1, nc.scalar.copy)
         add_bias(last, 0)
-        round_y(last - 1, 1, nc.vector.tensor_copy)
         add_bias(last, 1)
-        for k in biased:
-            finish_y(k)
+        finish_y(last - 2)
         round_y(last, 0, nc.vector.tensor_copy)
         round_y(last, 1, nc.vector.tensor_copy)
         finish_y(last - 1)
         for g in range(FG):
             gather_y(turn_words(y_bf[last], [g]), last, [g])
-        for k in biased + [last - 1]:
-            quantize_y(k)
+        quantize_y(last - 2)
+        quantize_y(last - 1)
         for g in range(FG):
             quantize_y(last, [g])
 

from contextlib import ExitStack

import concourse.mybir as mybir
from concourse.masks import make_identity

F32 = mybir.dt.float32
BF16 = mybir.dt.bfloat16
I32 = mybir.dt.int32
U32 = mybir.dt.uint32
U8 = mybir.dt.uint8
FP8X4 = mybir.dt.float8_e4m3fn_x4
FP4X4 = mybir.dt.float4_e2m1fn_x4
ADD = mybir.AluOpType.add
MULT = mybir.AluOpType.mult

P = 128
KP = 512
S, R, F = 1024, 1536, 1024
NI, NJ, NL = 16, 8, 8
TILES = S // P
RG = R // KP
FG = F // KP
PAIRS = TILES // 2
FLOPS = 2 * S * F * (R + F + F)
EARLY = 4
ON_VECTOR = (4, 5, 6)
ROUNDED_FIRST = (4, 5, 6, 7)
STAGE1_AT = {0: 5, 2: 6, 4: 7}
STAGE3_AT = {4: (0,), 5: (1, 2), 6: (3,), 7: (4, 5)}


def tile_cp_radiance_shading_k1_kernel(
    tc, fx, fy, fz, basis, x, view, w1_words, w1_scales, w2, b, out_0, out_1, out_2
):
    nc = tc.nc
    with ExitStack() as ctx:
        keep = ctx.enter_context(tc.tile_pool(name="keep", bufs=1))
        work = ctx.enter_context(tc.tile_pool(name="work", bufs=3))
        psum = ctx.enter_context(tc.psum_pool(name="psum", bufs=4))
        ctx.enter_context(tc.manual_schedule())

        fac = keep.tile([P, R], BF16, name="fac")
        nc.vector.memset(fac[32:64, :].bitcast(I32), 0)
        nc.vector.memset(fac[64:128, :].bitcast(I32), 0)
        ident = keep.tile([P, P], F32, name="ident")
        make_identity(nc, ident[:])
        w1_scale = keep.tile([P, FG, F], U8, name="w1_scale", align_bytes=64)
        nc.vector.memset(w1_scale[:].rearrange("p g n -> p (g n)").bitcast(I32), 0)

        nc.sync.dma_start(out=fac[16:24, :], in_=fy)
        nc.sync.dma_start(out=fac[24:32, :], in_=fz)
        nc.sync.dma_start(out=fac[0:16, :], in_=fx)

        def load_weight(w, g, h, name):
            raw = work.tile([P, 4, KP], BF16, name=name, tag="raw", bufs=6)
            nc.sync.dma_start(
                out=raw[:], in_=w[KP * g : KP * (g + 1), KP * h : KP * (h + 1)].rearrange("(p t) n -> p t n", t=4)
            )
            return raw

        def load_rows(a, c, name):
            rows = keep.tile([P, 2, F], BF16, name=name)
            nc.sync.dma_start(out=rows[:], in_=a[2 * P * c : 2 * P * (c + 1), :].rearrange("(j p) f -> p j f", p=P))
            return rows

        basis_raw = {}
        for h in range(FG):
            for g in range(RG):
                basis_raw[g, h] = load_weight(basis, g, h, "basis_raw%d%d" % (g, h))
        x_sb = {c: load_rows(x, c, "x%d" % c) for c in range(2)}
        w1_code = keep.tile([P, FG, 2 * F], U8, name="w1_code", align_bytes=64)
        bias = keep.tile([P, F], BF16, name="bias")
        view_sb, w2_raw = {}, {}

        def later_loads():
            for h in range(FG):
                for g in range(FG):
                    w2_raw[g, h] = load_weight(w2, g, h, "w2_raw%d%d" % (g, h))
            x_sb[2] = load_rows(x, 2, "x2")
            for q in range(4):
                nc.sync.dma_start(
                    out=w1_scale[32 * q : 32 * q + 4, :, :].bitcast(I32),
                    in_=w1_scales[:, 4 * q : 4 * q + 4, :].rearrange("g r n -> r g n").bitcast(I32),
                )
            nc.sync.dma_start(out=w1_code[:].bitcast(I32), in_=w1_words.rearrange("g p n -> p g n").bitcast(I32))
            view_sb[0] = load_rows(view, 0, "view0")
            x_sb[3] = load_rows(x, 3, "x3")
            for c in range(1, PAIRS):
                view_sb[c] = load_rows(view, c, "view%d" % c)
            nc.sync.dma_start(out=bias[:], in_=b.partition_broadcast(P))

        fac_words = fac[:].bitcast(F32)
        fac_t = []
        fyz = []
        fac_banks = []
        for g in range(RG):
            fac_bank = psum.tile([P, KP], F32, name="fac_bank", tag="tr")
            for u in range(2):
                nc.tensor.transpose(fac_bank[:, P * u : P * (u + 1)], fac_words[:, 256 * g + u : 256 * (g + 1) : 2], ident[:])
            fac_banks.append(fac_bank)

        def axis_factors(g):
            ft = keep.tile([P, 32, 4], BF16, name="fac_t%d" % g)
            nc.vector.tensor_copy(
                out=ft[:].rearrange("p r t -> p (r t)").bitcast(F32).rearrange("p (r u) -> p r u", u=2),
                in_=fac_banks[g][:, 0 : 2 * P].rearrange("p (u r) -> p r u", u=2)[:, 0:32, :],
            )
            fac_t.append(ft)

        def outer_yz(g):
            yz = keep.tile([P, NJ, NL, 4], F32, name="fyz%d" % g)
            nc.vector.tensor_tensor(
                out=yz[:],
                in0=fac_t[g][:, 16:24, :].unsqueeze(2).to_broadcast([P, NJ, NL, 4]),
                in1=fac_t[g][:, 24:32, :].unsqueeze(1).to_broadcast([P, NJ, NL, 4]),
                op=MULT,
            )
            fyz.append(yz)

        def quantize(src, name, pool, bufs=None):
            width = src.shape[1] // 4
            code = pool.tile([P, width], U32, name=name + "_code", align_bytes=64, bufs=bufs)
            scale = pool.tile([P, width], U8, name=name + "_scale", align_bytes=64, bufs=bufs)
            nc.vector.quantize_mx(out=code[:].bitcast(FP8X4), scales=scale[:], in_=src)
            return code, scale

        def interleave(copy, raw, grouped, first, last):
            copy(
                out=grouped[:, 4 * first : 4 * last].rearrange("p (c i t) -> p c t i", i=4, t=4),
                in_=raw[:, :, first:last].rearrange("p t (c i) -> p c t i", i=4),
            )

        def new_grouped():
            return work.tile([P, KP * 4], BF16, name="grouped", align_bytes=64, bufs=3)

        h_bf, h_q, basis_q, w2_q = {}, {}, {}, {}

        def make_h(first, count, g):
            hb = work.tile([P, 2 * count, NJ * NL, 4], BF16, name="h_bf", align_bytes=64, bufs=3)
            shape = [P, 2 * count, NJ * NL, 4]
            nc.vector.tensor_tensor(
                out=hb[:],
                in0=fyz[g][:].rearrange("p j l t -> p (j l) t").unsqueeze(1).to_broadcast(shape),
                in1=fac_t[g][:, 2 * first : 2 * (first + count), :].unsqueeze(2).to_broadcast(shape),
                op=MULT,
            )
            h_bf[first, g] = hb

        def quantize_h(first, count, g):
            code, scale = quantize(h_bf[first, g][:].rearrange("p i m t -> p (i m t)"), "h", work, bufs=2 * RG + 1)
            for k in range(count):
                h_q[first + k, g] = (code[:, P * k : P * (k + 1)], scale[:, P * k : P * (k + 1)])

        def mx_passes(acts, weights):
            bank = psum.tile([P, KP], F32, name="mx_bank", tag="mx")
            for n in range(len(acts)):
                nc.tensor.matmul_mx(
                    out=bank[:],
                    lhsT=acts[n][0].bitcast(FP8X4),
                    lhsT_scale=acts[n][1],
                    rhs=weights[n][0],
                    rhs_scale=weights[n][1],
                    start=(n == 0),
                    stop=(n == len(acts) - 1),
                )
            return bank

        def act_passes(q):
            return [(q[0][:, P * g : P * (g + 1)], q[1][:, P * g : P * (g + 1)]) for g in range(FG)]

        def sorted_view(ap, j):
            if j in ON_VECTOR:
                return ap.rearrange("p (u q e) -> p u q e", u=2, e=2)
            return ap.rearrange("p (t c i) -> p c t i", t=4, i=4)

        def plain_view(ap, j):
            if j in ON_VECTOR:
                return ap.rearrange("p (q u e) -> p u q e", u=2, e=2)
            return ap.rearrange("p (c i t) -> p c t i", t=4, i=4)

        bank1, bank2, bank3, tr1, tr2, tr3 = {}, {}, {}, {}, {}, {}
        u1, mod, y, u1_bf, u2_bf, y_bf, yt_bf, u1_q, u2_q = {}, {}, {}, {}, {}, {}, {}, {}, {}
        u1_w, u2_w = {}, {}
        y_code = {}
        y_scale = keep.tile([P, FG, S], U8, name="y_scale", align_bytes=64)

        def live(j):
            return 0 <= j < TILES

        def stage1(j, h):
            bank1[j, h] = mx_passes(
                [h_q[j, g] for g in range(RG)],
                [(basis_q[g, h][0][:].bitcast(FP8X4), basis_q[g, h][1][:]) for g in range(RG)],
            )

        def add_x(j, h):
            if h == 0:
                u1[j] = work.tile([P, F], F32, name="u1", bufs=6)
            cols = slice(KP * h, KP * (h + 1))
            nc.vector.tensor_tensor(
                out=sorted_view(u1[j][:, cols], j),
                in0=plain_view(bank1[j, h][:], j),
                in1=plain_view(x_sb[j // 2][:, j % 2, cols], j),
                op=ADD,
            )

        def add_u2(j, g):
            if g == 0:
                u2_w[j] = work.tile([P, F], BF16, name="u2_w", bufs=2)
            cols = slice(KP * g, KP * (g + 1))
            nc.vector.tensor_tensor(out=u2_w[j][:, cols], in0=u1[j][:, cols], in1=mod[j][:, cols], op=ADD)

        def round_u1(j, g):
            if g == 0:
                u1_w[j] = work.tile([P, F], BF16, name="u1_w", bufs=2)
            cols = slice(KP * g, KP * (g + 1))
            if j in ON_VECTOR:
                nc.scalar.copy(out=u1_w[j][:, cols], in_=u1[j][:, cols])
            else:
                nc.scalar.copy(
                    out=u1_w[j][:, cols].rearrange("p (u q e) -> p u q e", u=2, e=2),
                    in_=u1[j][:, cols].rearrange("p (u e q) -> p u q e", u=2, e=2),
                )

        def turn_u1_half(j, g):
            bank = psum.tile([P, KP], F32, name="tr_bank", tag="tr")
            for t in range(4):
                cols = slice(KP * g + P * t, KP * g + P * (t + 1))
                nc.tensor.transpose(bank[:, P * t : P * (t + 1)], u1[j][:, cols], ident[:])
            tr1[j, g] = bank
            round_turned(u1_bf, tr1, j, g, "u1_bf", 5)

        def turn_words(src, groups=range(FG)):
            bank = psum.tile([P, KP], F32, name="tr_bank", tag="tr")
            words = src[:].bitcast(F32)
            for g in groups:
                for n in (2 * g, 2 * g + 1):
                    nc.tensor.transpose(bank[:, P * n : P * (n + 1)], words[:, P * n : P * (n + 1)], ident[:])
            return bank

        def gather_words(bank, name, bufs=2):
            dst = work.tile([P, F], BF16, name=name, align_bytes=64, bufs=bufs)
            nc.scalar.copy(
                out=dst[:].bitcast(F32).rearrange("p (g s u) -> p g s u", g=FG, u=2),
                in_=bank[:].rearrange("p (g u s) -> p g s u", g=FG, u=2),
            )
            return dst

        def plane_batch(j):
            return (j - j % 2, 2) if j < TILES - 2 else (j, 1)

        def gather_y(bank, j, groups):
            first, count = plane_batch(j)
            if first not in yt_bf:
                yt_bf[first] = work.tile([P, FG, count * KP], BF16, name="yt_bf", align_bytes=64, bufs=3)
            gs = slice(groups[0], groups[-1] + 1)
            nc.scalar.copy(
                out=yt_bf[first][:, gs, KP * (j - first) : KP * (j - first + 1)]
                .bitcast(F32)
                .rearrange("p g (s u) -> p g s u", u=2),
                in_=bank[:].rearrange("p (g u s) -> p g s u", g=FG, u=2)[:, gs, :, :],
            )

        def round_turned(dst, banks, j, g, name, bufs):
            if g == 0:
                dst[j] = work.tile([P, F], BF16, name=name, align_bytes=64, bufs=bufs)
            nc.scalar.copy(
                out=dst[j][:, KP * g : KP * (g + 1)].rearrange("p (s t) -> p s t", t=4),
                in_=banks[j, g][:].rearrange("p (t s) -> p s t", t=4),
            )

        def stage2(j, h):
            bank2[j, h] = mx_passes(
                act_passes(u1_q[j]),
                [
                    (w1_code[:, g, 2 * KP * h : 2 * KP * (h + 1)].bitcast(FP4X4), w1_scale[:, g, KP * h : KP * (h + 1)])
                    for g in range(FG)
                ],
            )

        def mul_view(j, h):
            if h == 0:
                mod[j] = work.tile([P, F], F32, name="mod", bufs=3)
            cols = slice(KP * h, KP * (h + 1))
            nc.vector.tensor_tensor(
                out=sorted_view(mod[j][:, cols], j),
                in0=plain_view(bank2[j, h][:], j),
                in1=plain_view(view_sb[j // 2][:, j % 2, cols], j),
                op=MULT,
            )

        def turn_u2(j, g):
            bank = psum.tile([P, KP], F32, name="tr_bank", tag="tr")
            for t in range(4):
                cols = slice(KP * g + P * t, KP * g + P * (t + 1))
                out = bank[:, P * t : P * (t + 1)]
                nc.tensor.matmul(out, lhsT=u1[j][:, cols], rhs=ident[:], is_transpose=True, start=True, stop=False)
                nc.tensor.matmul(out, lhsT=mod[j][:, cols], rhs=ident[:], is_transpose=True, start=False, stop=True)
            tr2[j, g] = bank

        def stage3(j, h):
            bank3[j, h] = mx_passes(
                act_passes(u2_q[j]),
                [(w2_q[g, h][0][:].bitcast(FP8X4), w2_q[g, h][1][:]) for g in range(FG)],
            )

        def add_bias(j, h):
            if h == 0:
                y[j] = work.tile([P, F], F32, name="y", bufs=3)
            cols = slice(KP * h, KP * (h + 1))
            nc.vector.tensor_tensor(out=y[j][:, cols], in0=bank3[j, h][:], in1=bias[:, cols], op=ADD)
            if h == FG - 1:
                nc.sync.dma_start(out=out_0[P * j : P * (j + 1), :], in_=y[j][:])

        def round_y(j, g, copy):
            if g == 0:
                y_bf[j] = work.tile([P, F], BF16, name="y_bf", bufs=4)
            cols = slice(KP * g, KP * (g + 1))
            copy(
                out=y_bf[j][:, cols].rearrange("p (u q e) -> p u q e", u=2, e=2),
                in_=y[j][:, cols].rearrange("p (q u e) -> p u q e", u=2, e=2),
            )

        def quantize_y(j, groups=range(FG)):
            first, count = plane_batch(j)
            if j != first + count - 1:
                return
            if first not in y_code:
                y_code[first] = work.tile([P, FG, count * P], U32, name="y_code", align_bytes=64)
            for g in groups:
                nc.vector.quantize_mx(
                    out=y_code[first][:, g, :].bitcast(FP8X4),
                    scales=y_scale[:, g, P * first : P * (j + 1)],
                    in_=yt_bf[first][:, g, :],
                )
            if FG - 1 in groups:
                nc.sync.dma_start(
                    out=out_1.rearrange("g p m t -> p g (m t)").bitcast(I32)[:, :, P * first : P * (j + 1)],
                    in_=y_code[first][:].bitcast(I32),
                )

        h_todo = [(j, n, g) for j, n in ((0, 2), (2, 2), (4, 2), (6, 1), (7, 1)) for g in range(RG)]
        w2_todo = [(g, h, part) for h in range(FG) for g in range(FG) for part in range(2)]
        h_made, w2_made, w2_grouped, basis_grouped = [], [], {}, {}

        def next_h():
            if h_todo:
                piece = h_todo.pop(0)
                make_h(*piece)
                h_made.append(piece)

        def finish_h():
            while h_made:
                quantize_h(*h_made.pop(0))

        def quantize_basis(g, h):
            basis_q[g, h] = quantize(basis_grouped[g, h][:], "basis%d%d" % (g, h), keep)

        def group_basis(g, h):
            basis_grouped[g, h] = new_grouped()
            interleave(nc.scalar.copy, basis_raw[g, h], basis_grouped[g, h], 0, KP)

        def next_w2():
            if w2_todo:
                g, h, part = w2_todo.pop(0)
                if part == 0:
                    w2_grouped[g, h] = new_grouped()
                interleave(nc.scalar.copy, w2_raw[g, h], w2_grouped[g, h], part * KP // 2, (part + 1) * KP // 2)
                if part == 1:
                    w2_made.append((g, h))

        def finish_w2():
            while w2_made:
                piece = w2_made.pop(0)
                w2_q[piece] = quantize(w2_grouped[piece][:], "w2_%d%d" % piece, keep)

        def turn_u1(j):
            u1_bf[j] = gather_words(turn_words(u1_w[j]), "u1_bf", 5)

        def quantize_u1(j):
            u1_q[j] = quantize(u1_bf[j][:], "u1", work, bufs=6)

        def quantize_u2(j):
            u2_q[j] = quantize(u2_bf[j][:], "u2", work, bufs=5)

        def h_run(n):
            for k in range(n):
                next_h()
            finish_h()

        for g in range(RG):
            group_basis(g, 0)
        axis_factors(0)
        outer_yz(0)
        axis_factors(1)
        next_h()
        axis_factors(2)
        outer_yz(1)
        outer_yz(2)
        next_h()
        quantize_basis(0, 0)
        group_basis(0, 1)
        finish_h()
        next_h()
        quantize_basis(1, 0)
        group_basis(1, 1)
        finish_h()
        next_h()
        quantize_basis(2, 0)
        group_basis(2, 1)
        later_loads()
        stage1(0, 0)
        stage1(1, 0)
        finish_h()
        next_h()
        quantize_basis(0, 1)
        finish_h()
        next_h()
        add_x(0, 0)
        finish_h()
        stage1(2, 0)
        stage1(3, 0)
        quantize_basis(1, 1)
        add_x(1, 0)
        next_h()
        turn_u1_half(0, 0)
        turn_u1_half(1, 0)
        quantize_basis(2, 1)
        finish_h()
        next_w2()
        stage1(0, 1)
        stage1(1, 1)
        add_x(2, 0)
        add_x(3, 0)
        stage1(2, 1)
        stage1(3, 1)
        next_w2()
        add_x(0, 1)
        next_h()
        add_x(1, 1)
        next_h()
        finish_h()
        add_x(2, 1)
        add_x(3, 1)
        turn_u1_half(0, 1)
        turn_u1_half(2, 0)
        turn_u1_half(1, 1)
        turn_u1_half(3, 0)
        next_w2()
        stage1(4, 0)
        stage1(4, 1)
        quantize_u1(0)
        add_x(4, 0)
        finish_w2()
        quantize_u1(1)
        add_x(4, 1)
        turn_u1_half(2, 1)
        turn_u1_half(3, 1)
        next_w2()

        def finish_y(j):
            gather_y(turn_words(y_bf[j]), j, range(FG))

        def turn_sum(k):
            if k in ON_VECTOR:
                u2_bf[k] = gather_words(turn_words(u2_w[k]), "u2_bf")
            else:
                for g in range(FG):
                    turn_u2(k, g)
                    round_turned(u2_bf, tr2, k, g, "u2_bf", 2)

        biased, gathered, added, waiting = [], [], [4], [2, 3]
        for a in range(TILES):
            j = STAGE1_AT.get(a)
            stage2(a, 0)
            stage2(a, 1)
            for k in added:
                round_u1(k, 0)
                round_u1(k, 1)
            for k in biased:
                round_y(k, 0, nc.scalar.copy)
                round_y(k, 1, nc.scalar.copy)
            next_w2()
            rounded, added = added, []
            turned, biased = biased, []
            mul_view(a, 0)
            mul_view(a, 1)
            if j:
                stage1(j, 0)
                stage1(j, 1)
            if waiting:
                quantize_u1(waiting.pop(0))
            if j:
                add_x(j, 0)
            if live(a - 2):
                quantize_u2(a - 2)
            next_h()
            if j:
                add_x(j, 1)
                added.append(j)
            finish_w2()
            for c in STAGE3_AT.get(a, ()):
                stage3(c, 0)
                stage3(c, 1)
                add_bias(c, 0)
                add_bias(c, 1)
                biased.append(c)
            if j:
                next_h()
            for k in gathered:
                quantize_y(k)
            if a in ON_VECTOR:
                add_u2(a, 0)
                add_u2(a, 1)
            finish_h()
            if a == TILES - 1:
                round_y(biased[0], 0, nc.scalar.copy)
                round_y(biased[0], 1, nc.scalar.copy)
            if live(a - 1):
                turn_sum(a - 1)
            for k in rounded:
                turn_u1(k)
                waiting.append(k)
            for k in turned:
                finish_y(k)
            gathered = turned

        last = TILES - 1
        turn_sum(last)
        quantize_u2(last - 1)
        round_y(last - 2, 0, nc.vector.tensor_copy)
        round_y(last - 2, 1, nc.vector.tensor_copy)
        finish_y(last - 3)
        stage3(last - 1, 0)
        stage3(last - 1, 1)
        for k in gathered:
            quantize_y(k)
        quantize_u2(last)
        add_bias(last - 1, 0)
        add_bias(last - 1, 1)
        stage3(last, 0)
        stage3(last, 1)
        round_y(last - 1, 0, nc.scalar.copy)
        round_y(last - 1, 1, nc.scalar.copy)
        add_bias(last, 0)
        add_bias(last, 1)
        finish_y(last - 2)
        round_y(last, 0, nc.vector.tensor_copy)
        round_y(last, 1, nc.vector.tensor_copy)
        finish_y(last - 1)
        for g in range(FG):
            gather_y(turn_words(y_bf[last], [g]), last, [g])
        quantize_y(last - 2)
        quantize_y(last - 1)
        for g in range(FG):
            quantize_y(last, [g])

        for q in range(4):
            queue = nc.sync if q < 2 else nc.scalar
            queue.dma_start(
                out=out_2[:, 4 * q : 4 * q + 4, :].rearrange("g r m -> r g m").bitcast(I32),
                in_=y_scale[32 * q : 32 * q + 4, :, :].bitcast(I32),
            )
